import numpy as np
import ml_dtypes


def mxq(x, axis, fmt="e4m3"):
    dtype, down = {"e4m3": (ml_dtypes.float8_e4m3fn, 7), "e5m2": (ml_dtypes.float8_e5m2, 14)}[fmt]
    v = np.moveaxis(np.asarray(x, np.float32).astype(ml_dtypes.bfloat16).astype(np.float64), axis, -1)
    blocks = v.reshape(v.shape[:-1] + (-1, 32))
    amax = np.abs(blocks).max(-1, keepdims=True)
    byte = np.maximum(np.where(amax > 0, np.frexp(amax)[1] - 1 + 127, 0) - down, 1)
    scale = np.exp2(byte - 127.0)
    codes = (blocks / scale).astype(np.float32).astype(dtype).astype(np.float64)
    return np.moveaxis((codes * scale).reshape(v.shape), -1, axis)


WIDE = False


def mx_kscale(k):
    if not WIDE:
        return np.ones(k)
    levels = np.array([10, -10, 5, -5, 0])
    if k % 512:
        return np.exp2(np.random.permutation(np.resize(levels, k // 32))).repeat(32)
    a = np.empty((k // 512, 16))
    for p in range(k // 512):
        a[p, :8] = np.random.permutation(np.resize(levels, 8))
        for g in range(8):
            far = levels[np.abs(levels - a[p, g]) >= 10]
            a[p, g + 8] = far[np.random.randint(len(far))]
    return np.exp2(a.ravel()).repeat(32)


def f64(x):
    return np.asarray(x).astype(np.float64)


def striped(idx):
    return np.tile(idx.reshape(-1, 16).T, (8, 1)).astype(np.uint16)


def unstriped(offs):
    return offs[:16].T.reshape(-1).astype(np.int64)


E2M1 = np.array([0.0, 0.5, 1.0, 1.5, 2.0, 3.0, 4.0, 6.0, -0.0, -0.5, -1.0, -1.5, -2.0, -3.0, -4.0, -6.0])


def pack_weight(w, fmt):
    k, n = w.shape
    w = f64(np.asarray(w, np.float32).astype(ml_dtypes.bfloat16)).reshape(k // 32, 32, n)
    amax = np.abs(w).max(1)
    if fmt == "e4m3":
        byte = np.frexp(amax)[1] - 1 + 127 - 7
    else:
        mant, ex = np.frexp(amax / 6.0)
        byte = np.where(mant > 0.5, ex, ex - 1) + 127
    byte = np.clip(np.where(amax > 0, byte, 1), 1, 254)
    scaled = (w * np.exp2(127.0 - byte)[:, None, :]).reshape(k, n).astype(np.float32)
    by_word = np.ascontiguousarray(scaled.reshape(k // 512, 128, 4, n).transpose(0, 1, 3, 2))
    if fmt == "e4m3":
        words = by_word.astype(ml_dtypes.float8_e4m3fn).view(np.uint8)
    else:
        c = by_word.astype(ml_dtypes.float4_e2m1fn).view(np.uint8) & 0xF
        words = (c[..., 0::2] | (c[..., 1::2] << 4)).reshape(k // 512, 128, 2 * n)
    return np.ascontiguousarray(words), np.ascontiguousarray(byte.astype(np.uint8).reshape(k // 512, 16, n))


def unpack_weight(words, scales, fmt):
    g, _, n = scales.shape
    words = np.ascontiguousarray(words).reshape(g, 128, n, -1)
    if fmt == "e4m3":
        vals = words.view(ml_dtypes.float8_e4m3fn).astype(np.float64)
    else:
        nib = np.empty((g, 128, n, 4), np.uint8)
        nib[..., 0::2] = words & 0xF
        nib[..., 1::2] = words >> 4
        vals = E2M1[nib]
    vals = vals * np.repeat(np.exp2(scales.astype(np.float64) - 127.0), 8, axis=1)[..., None]
    return vals.transpose(0, 1, 3, 2).reshape(g * 512, n)


def gelu(v):
    return 0.5 * v * (1.0 + np.tanh(np.sqrt(2.0 / np.pi) * (v + 0.044715 * v**3)))


K, H, N, T, S, T2, P = 1024, 512, 768, 4096, 1024, 2048, 1024


def setup_inputs():
    n = np.random.standard_normal
    s = mx_kscale(K)[:, None]
    u = mx_kscale(H)[:, None]
    tab_words, tab_scales = pack_weight(n((K, T)) * s, "e4m3")
    w2_words, w2_scales = pack_weight(n((K, H)) / np.sqrt(K) / s * u.T, "e2m1")
    w4_words, w4_scales = pack_weight(n((H, N)) / np.sqrt(H) / u, "e4m3")
    return {
        "tab_words": tab_words,
        "tab_scales": tab_scales,
        "offs": striped(np.random.permutation(T)[:S]),
        "offs2": striped(np.random.permutation(T2)[:S]),
        "offs3": striped(np.random.permutation(T2)[:P]),
        "w1": (n((K, H)) / np.sqrt(K) / s * u.T).astype(np.float32),
        "w2_words": w2_words,
        "w2_scales": w2_scales,
        "b2": (0.5 * n(H) * u[:, 0]).astype(np.float32),
        "page0": (n((H, T2)) * u).astype(np.float32),
        "w3": (1.2 * n((H, N)) / np.sqrt(H) / u).astype(np.float32),
        "d": np.random.uniform(0.8, 2.0, N).astype(np.float32),
        "w4_words": w4_words,
        "w4_scales": w4_scales,
    }


def reference(tab_words, tab_scales, offs, offs2, offs3, w1, w2_words, w2_scales, b2, page0, w3, d, w4_words, w4_scales):
    v = unpack_weight(tab_words, tab_scales, "e4m3")[:, unstriped(offs)]
    h1 = mxq(f64(w1), 0, "e4m3").T @ v
    h2 = (unpack_weight(w2_words, w2_scales, "e2m1").T @ v) + f64(b2)[:, None]
    page = f64(page0).copy()
    l2 = unstriped(offs2)
    page[:, l2] = np.maximum(page[:, l2] + h1, h2)
    x = mxq(page[:, unstriped(offs3)], 0, "e4m3")
    y1 = mxq(f64(w3), 0, "e4m3").T @ x
    y2 = unpack_weight(w4_words, w4_scales, "e4m3").T @ x
    return f64(d)[:, None] * np.tanh(y1) + y2

@@ -1,0 +1,244 @@
+from contextlib import ExitStack
+
+import concourse.mybir as mybir
+
+K, H, N, T, S, T2, PICKS = 1024, 512, 768, 4096, 1024, 2048, 1024
+FLOPS = 2 * 2 * K * H * S + 2 * 2 * H * N * PICKS
+
+F32 = mybir.dt.float32
+BF16 = mybir.dt.bfloat16
+I32 = mybir.dt.int32
+U32 = mybir.dt.uint32
+U16 = mybir.dt.uint16
+U8 = mybir.dt.uint8
+FP8X4 = mybir.dt.float8_e4m3fn_x4
+FP4X4 = mybir.dt.float4_e2m1fn_x4
+ADD = mybir.AluOpType.add
+MULT = mybir.AluOpType.mult
+MAX = mybir.AluOpType.max
+TANH = mybir.ActivationFunctionType.Tanh
+
+P = 128
+PACK = 4
+PASSES = K // (P * PACK)
+BANK = 512
+HALVES = S // BANK
+CHUNK = 256
+CHUNKS = PICKS // CHUNK
+N_TILES = N // P
+PER_COL = 16
+
+
+def tile_list_bin_habit_update_kernel(
+    tc, tab_words, tab_scales, offs, offs2, offs3, w1, w2_words, w2_scales, b2, page0, w3, d, w4_words, w4_scales, out
+):
+    nc = tc.nc
+    with ExitStack() as ctx:
+        keep = ctx.enter_context(tc.tile_pool(name="keep", bufs=1))
+        ring = ctx.enter_context(tc.tile_pool(name="ring", bufs=2))
+        outs = ctx.enter_context(tc.tile_pool(name="outs", bufs=4))
+        psum = ctx.enter_context(tc.psum_pool(name="psum", bufs=4))
+
+        def held(shape, dtype, name):
+            return keep.tile(shape, dtype, name=name, align_bytes=64)
+
+        lift_list = held([P, S // PER_COL], U16, "lift_list")
+        put_list = held([P, S // PER_COL], U16, "put_list")
+        read_list = held([P, PICKS // PER_COL], U16, "read_list")
+        tab_w = [held([P, T], I32, f"tab_w{a}") for a in range(PASSES)]
+        tab_s = held([P, PASSES * T], U8, "tab_s")
+        v_w = [held([P, S], U32, f"v_w{a}") for a in range(PASSES)]
+        v_s = held([P, PASSES * S], U8, "v_s")
+        w1_raw = [held([P, PACK * H], F32, f"w1_raw{a}") for a in range(PASSES)]
+        w1_bf = [held([P, PACK * H], BF16, f"w1_bf{a}") for a in range(PASSES)]
+        w1_w = [held([P, H], U32, f"w1_w{a}") for a in range(PASSES)]
+        w1_s = [held([P, H], U8, f"w1_s{a}") for a in range(PASSES)]
+        w2_raw_w = held([P, PASSES * 2 * H], U8, "w2_raw_w")
+        w2_raw_s = held([P, PASSES * H], U8, "w2_raw_s")
+        w2_w = held([P, PASSES * 2 * H], U8, "w2_w")
+        w2_s = held([P, PASSES * H], U8, "w2_s")
+        b2_col = held([P, PACK], F32, "b2_col")
+        d_col = held([P, N_TILES], F32, "d_col")
+        page = [held([P, T2], F32, f"page{t}") for t in range(PACK)]
+        w3_raw = held([P, PACK * N], F32, "w3_raw")
+        w3_bf = held([P, PACK * N], BF16, "w3_bf")
+        w3_w = held([P, N], U32, "w3_w")
+        w3_s = held([P, N], U8, "w3_s")
+        w4_w = held([P, N], I32, "w4_w")
+        w4_s = held([P, N], U8, "w4_s")
+
+        nc.vector.memset(tab_s[:].bitcast(I32), 0)
+        nc.gpsimd.memset(w2_raw_s[:].bitcast(I32), 0)
+        nc.gpsimd.memset(w4_s[:].bitcast(I32), 0)
+
+        def load_scales(plane, scales):
+            passes = scales.shape[0]
+            for q in range(4):
+                nc.sync.dma_start(
+                    out=plane[32 * q : 32 * q + 4, :].bitcast(I32).rearrange("r (a n) -> r a n", a=passes),
+                    in_=scales[:, 4 * q : 4 * q + 4, :].bitcast(I32).rearrange("a r n -> r a n"),
+                )
+
+        def load_table(a):
+            nc.sync.dma_start(out=tab_w[a][:], in_=tab_words[a].rearrange("p n i -> p (n i)").bitcast(I32))
+
+        nc.sync.dma_start(lift_list[:], offs)
+        load_table(0)
+        load_scales(tab_s, tab_scales)
+        for a in range(PASSES):
+            nc.sync.dma_start(
+                out=w1_raw[a][:], in_=w1[a * P * PACK : (a + 1) * P * PACK, :].rearrange("(p j) c -> p (j c)", j=PACK)
+            )
+        nc.sync.dma_start(
+            out=w2_raw_w[:].bitcast(I32).rearrange("p (a n) -> p a n", a=PASSES),
+            in_=w2_words.bitcast(I32).rearrange("a p n -> p a n"),
+        )
+        load_scales(w2_raw_s, w2_scales)
+        load_table(1)
+        nc.sync.dma_start(put_list[:], offs2)
+        nc.sync.dma_start(out=b2_col[:], in_=b2.rearrange("(p t) -> p t", t=PACK))
+        page_rows = page0.rearrange("(p t) c -> p t c", t=PACK)
+        for t in range(PACK):
+            nc.sync.dma_start(out=page[t][:], in_=page_rows[:, t, :])
+        nc.sync.dma_start(read_list[:], offs3)
+        nc.sync.dma_start(out=w3_raw[:], in_=w3.rearrange("(p j) c -> p (j c)", j=PACK))
+        nc.sync.dma_start(out=w4_w[:], in_=w4_words[0].rearrange("p n i -> p (n i)").bitcast(I32))
+        load_scales(w4_s, w4_scales)
+        with nc.allow_non_contiguous_dma(reason="one factor of d for each partition"):
+            nc.sync.dma_start(out=d_col[:], in_=d.rearrange("(c p) -> p c", p=P))
+
+        def list_part(lst, start, count):
+            return lst[:, start // PER_COL : (start + count) // PER_COL]
+
+        nc.vector.tensor_copy(out=v_w[0][:], in_=tab_w[0][:].bitcast(U32).indirect(lift_list[:]))
+        for a in range(PASSES):
+            nc.vector.tensor_copy(
+                out=v_s[:, a * S : (a + 1) * S], in_=tab_s[:, a * T : (a + 1) * T].indirect(lift_list[:])
+            )
+        for a in range(PASSES):
+            nc.scalar.copy(
+                out=w1_bf[a][:].rearrange("p (t m j) -> p m t j", t=PACK, j=PACK),
+                in_=w1_raw[a][:].rearrange("p (j m t) -> p m t j", t=PACK, j=PACK),
+            )
+            nc.vector.quantize_mx(out=w1_w[a][:].bitcast(FP8X4), scales=w1_s[a][:], in_=w1_bf[a][:])
+        nc.vector.tensor_copy(
+            out=w2_w[:].bitcast(U16).rearrange("p (a t m) -> p a t m", a=PASSES, t=PACK),
+            in_=w2_raw_w[:].bitcast(U16).rearrange("p (a m t) -> p a t m", a=PASSES, t=PACK),
+        )
+        nc.vector.tensor_copy(
+            out=w2_s[:].rearrange("p (a t m) -> p a t m", a=PASSES, t=PACK),
+            in_=w2_raw_s[:].rearrange("p (a m t) -> p a t m", a=PASSES, t=PACK),
+        )
+        for half in range(HALVES):
+            nc.vector.tensor_copy(
+                out=v_w[1][:, half * BANK : (half + 1) * BANK],
+                in_=tab_w[1][:].bitcast(U32).indirect(list_part(lift_list, half * BANK, BANK)),
+            )
+
+        for t in range(PACK):
+            h1 = ring.tile([P, S], F32, name="h1", tag="h1")
+            summed = ring.tile([P, S], F32, name="summed", tag="summed")
+            fresh = ring.tile([P, S], F32, name="fresh", tag="fresh")
+            h2_banks = []
+            for half in range(HALVES):
+                cols = slice(half * BANK, (half + 1) * BANK)
+                h1_bank = psum.tile([P, BANK], F32, name="h1_bank", tag="first")
+                h2_bank = psum.tile([P, BANK], F32, name="h2_bank", tag="second")
+                h2_banks.append(h2_bank)
+                for a in range(PASSES):
+                    nc.tensor.matmul_mx(
+                        out=h1_bank[:],
+                        lhsT=w1_w[a][:, t * P : (t + 1) * P].bitcast(FP8X4),
+                        lhsT_scale=w1_s[a][:, t * P : (t + 1) * P],
+                        rhs=v_w[a][:, cols].bitcast(FP8X4),
+                        rhs_scale=v_s[:, a * S + half * BANK : a * S + (half + 1) * BANK],
+                        start=(a == 0),
+                        stop=(a == PASSES - 1),
+                    )
+                for a in range(PASSES):
+                    first = a * H + t * P
+                    nc.tensor.matmul_mx(
+                        out=h2_bank[:],
+                        lhsT=w2_w[:, 2 * first : 2 * (first + P)].bitcast(FP4X4),
+                        lhsT_scale=w2_s[:, first : first + P],
+                        rhs=v_w[a][:, cols].bitcast(FP8X4),
+                        rhs_scale=v_s[:, a * S + half * BANK : a * S + (half + 1) * BANK],
+                        start=(a == 0),
+                        stop=(a == PASSES - 1),
+                    )
+                nc.scalar.copy(out=h1[:, cols], in_=h1_bank[:])
+                nc.vector.tensor_tensor(
+                    out=summed[:, cols],
+                    in0=page[t][:].indirect(list_part(put_list, half * BANK, BANK)),
+                    in1=h1[:, cols],
+                    op=ADD,
+                )
+            for half in range(HALVES):
+                cols = slice(half * BANK, (half + 1) * BANK)
+                nc.vector.scalar_tensor_tensor(
+                    out=fresh[:, cols],
+                    in0=h2_banks[half][:],
+                    scalar=b2_col[:, t : t + 1],
+                    in1=summed[:, cols],
+                    op0=ADD,
+                    op1=MAX,
+                )
+            nc.vector.tensor_copy(out=page[t][:].indirect(put_list[:]), in_=fresh[:])
+
+        nc.scalar.copy(
+            out=w3_bf[:].rearrange("p (c i j) -> p c j i", i=PACK, j=PACK),
+            in_=w3_raw[:].rearrange("p (j c i) -> p c j i", i=PACK, j=PACK),
+        )
+        for part in range(2):
+            cols = slice(part * N // 2, (part + 1) * N // 2)
+            nc.vector.quantize_mx(
+                out=w3_w[:, cols].bitcast(FP8X4),
+                scales=w3_s[:, cols],
+                in_=w3_bf[:, part * PACK * N // 2 : (part + 1) * PACK * N // 2],
+            )
+
+        out_rows = out.rearrange("(c p) m -> p c m", p=P)
+        for chunk in range(CHUNKS):
+            picked = ring.tile([P, PACK, CHUNK], F32, name="picked", tag=("summed", "fresh")[chunk % 2])
+            for t in range(PACK):
+                nc.vector.tensor_copy(
+                    out=picked[:, t, :], in_=page[t][:].indirect(list_part(read_list, chunk * CHUNK, CHUNK))
+                )
+            x_bf = ring.tile([P, CHUNK * PACK], BF16, name="x_bf", tag="x_bf", align_bytes=64)
+            x_w = ring.tile([P, CHUNK], U32, name="x_w", tag="x_w", align_bytes=64)
+            x_s = ring.tile([P, CHUNK], U8, name="x_s", tag="x_s", align_bytes=64)
+            nc.scalar.copy(
+                out=x_bf[:].rearrange("p (c i t) -> p c t i", i=PACK, t=PACK),
+                in_=picked[:].rearrange("p t (c i) -> p c t i", i=PACK),
+            )
+            nc.vector.quantize_mx(out=x_w[:].bitcast(FP8X4), scales=x_s[:], in_=x_bf[:])
+            for pair in range(N_TILES // 2):
+                y1_bank = psum.tile([P, 2, CHUNK], F32, name="y1_bank", tag="first")
+                y2_bank = psum.tile([P, 2, CHUNK], F32, name="y2_bank", tag="second")
+                for bank, words, scales in ((y1_bank, w3_w, w3_s), (y2_bank, w4_w, w4_s)):
+                    for side in range(2):
+                        cols = slice((2 * pair + side) * P, (2 * pair + side + 1) * P)
+                        nc.tensor.matmul_mx(
+                            out=bank[:, side, :],
+                            lhsT=words[:, cols].bitcast(FP8X4),
+                            lhsT_scale=scales[:, cols],
+                            rhs=x_w[:].bitcast(FP8X4),
+                            rhs_scale=x_s[:],
+                            start=True,
+                            stop=True,
+                        )
+                squashed = outs.tile([P, 2, CHUNK], F32, name="squashed", tag="squashed")
+                result = outs.tile([P, 2, CHUNK], F32, name="result", tag="result")
+                nc.scalar.activation(out=squashed[:], in_=y1_bank[:], func=TANH)
+                for side in range(2):
+                    nc.vector.scalar_tensor_tensor(
+                        out=result[:, side, :],
+                        in0=squashed[:, side, :],
+                        scalar=d_col[:, 2 * pair + side : 2 * pair + side + 1],
+                        in1=y2_bank[:, side, :],
+                        op0=MULT,
+                        op1=ADD,
+                    )
+                nc.sync.dma_start(
+                    out=out_rows[:, 2 * pair : 2 * pair + 2, chunk * CHUNK : (chunk + 1) * CHUNK], in_=result[:]
+                )

@@ -1,6 +1,7 @@
 from contextlib import ExitStack
 
 import concourse.mybir as mybir
+from concourse.masks import make_identity
 
 K, H, N, T, S, T2, PICKS = 1024, 512, 768, 4096, 1024, 2048, 1024
 FLOPS = 2 * 2 * K * H * S + 2 * 2 * H * N * PICKS
@@ -15,7 +16,9 @@ FP8X4 = mybir.dt.float8_e4m3fn_x4
 FP4X4 = mybir.dt.float4_e2m1fn_x4
 ADD = mybir.AluOpType.add
 MULT = mybir.AluOpType.mult
-MAX = mybir.AluOpType.max
+IDENTITY = mybir.ActivationFunctionType.Identity
+COPY = mybir.ActivationFunctionType.Copy
+RELU = mybir.ActivationFunctionType.Relu
 TANH = mybir.ActivationFunctionType.Tanh
 
 P = 128
@@ -23,10 +26,12 @@ PACK = 4
 PASSES = K // (P * PACK)
 BANK = 512
 HALVES = S // BANK
+BLOCKS = BANK // P
 CHUNK = 256
 CHUNKS = PICKS // CHUNK
 N_TILES = N // P
 PER_COL = 16
+PICKED_TAGS = ("floor2", "excess2", "floor3", "floor2")
 
 
 def tile_list_bin_habit_update_kernel(
@@ -37,7 +42,7 @@ def tile_list_bin_habit_update_kernel(
         keep = ctx.enter_context(tc.tile_pool(name="keep", bufs=1))
         ring = ctx.enter_context(tc.tile_pool(name="ring", bufs=2))
         outs = ctx.enter_context(tc.tile_pool(name="outs", bufs=4))
-        psum = ctx.enter_context(tc.psum_pool(name="psum", bufs=4))
+        psum = ctx.enter_context(tc.psum_pool(name="psum", bufs=2))
 
         def held(shape, dtype, name):
             return keep.tile(shape, dtype, name=name, align_bytes=64)
@@ -62,14 +67,16 @@ def tile_list_bin_habit_update_kernel(
         page = [held([P, T2], F32, f"page{t}") for t in range(PACK)]
         w3_raw = held([P, PACK * N], F32, "w3_raw")
         w3_bf = held([P, PACK * N], BF16, "w3_bf")
-        w3_w = held([P, N], U32, "w3_w")
         w3_s = held([P, N], U8, "w3_s")
         w4_w = held([P, N], I32, "w4_w")
         w4_s = held([P, N], U8, "w4_s")
 
+        ident = held([P, P], F32, "ident")
+
         nc.vector.memset(tab_s[:].bitcast(I32), 0)
         nc.gpsimd.memset(w2_raw_s[:].bitcast(I32), 0)
         nc.gpsimd.memset(w4_s[:].bitcast(I32), 0)
+        make_identity(nc, ident[:])
 
         def load_scales(plane, scales):
             passes = scales.shape[0]
@@ -136,25 +143,22 @@ def tile_list_bin_habit_update_kernel(
             )
 
         for t in range(PACK):
-            h1 = ring.tile([P, S], F32, name="h1", tag="h1")
-            summed = ring.tile([P, S], F32, name="summed", tag="summed")
-            fresh = ring.tile([P, S], F32, name="fresh", tag="fresh")
-            h2_banks = []
+            neg_old = ring.tile([P, S], F32, name="neg_old", tag="neg_old", bufs=PACK)
+            neg_h1 = ring.tile([P, S], F32, name="neg_h1", tag="neg_h1")
+            floor = ring.tile([P, S], F32, name="floor", tag=f"floor{t}", bufs=1, align_bytes=64)
+            excess = ring.tile([P, S], F32, name="excess", tag=f"excess{t}", bufs=1, align_bytes=64)
             for half in range(HALVES):
                 cols = slice(half * BANK, (half + 1) * BANK)
-                h1_bank = psum.tile([P, BANK], F32, name="h1_bank", tag="first")
-                h2_bank = psum.tile([P, BANK], F32, name="h2_bank", tag="second")
-                h2_banks.append(h2_bank)
-                for a in range(PASSES):
-                    nc.tensor.matmul_mx(
-                        out=h1_bank[:],
-                        lhsT=w1_w[a][:, t * P : (t + 1) * P].bitcast(FP8X4),
-                        lhsT_scale=w1_s[a][:, t * P : (t + 1) * P],
-                        rhs=v_w[a][:, cols].bitcast(FP8X4),
-                        rhs_scale=v_s[:, a * S + half * BANK : a * S + (half + 1) * BANK],
-                        start=(a == 0),
-                        stop=(a == PASSES - 1),
-                    )
+                nc.vector.tensor_scalar(
+                    out=neg_old[:, cols],
+                    in0=page[t][:].indirect(list_part(put_list, half * BANK, BANK)),
+                    scalar1=-1.0,
+                    scalar2=0.0,
+                    op0=MULT,
+                    op1=ADD,
+                )
+                h1_bank = psum.tile([P, BANK], F32, name="h1_bank", tag="h1")
+                h2_bank = psum.tile([P, BANK], F32, name="h2_bank", tag="h2")
                 for a in range(PASSES):
                     first = a * H + t * P
                     nc.tensor.matmul_mx(
@@ -166,25 +170,48 @@ def tile_list_bin_habit_update_kernel(
                         start=(a == 0),
                         stop=(a == PASSES - 1),
                     )
-                nc.scalar.copy(out=h1[:, cols], in_=h1_bank[:])
+                for a in range(PASSES):
+                    nc.tensor.matmul_mx(
+                        out=h1_bank[:],
+                        lhsT=w1_w[a][:, t * P : (t + 1) * P].bitcast(FP8X4),
+                        lhsT_scale=w1_s[a][:, t * P : (t + 1) * P],
+                        rhs=v_w[a][:, cols].bitcast(FP8X4),
+                        rhs_scale=v_s[:, a * S + half * BANK : a * S + (half + 1) * BANK],
+                        start=(a == 0),
+                        stop=(a == PASSES - 1),
+                    )
+                nc.scalar.activation(out=floor[:, cols], in_=h2_bank[:], func=IDENTITY, bias=b2_col[:, t : t + 1])
+                nc.scalar.activation(out=neg_h1[:, cols], in_=h1_bank[:], func=COPY, scale=-1.0)
+                gap_bank = psum.tile([P, BANK], F32, name="gap_bank", tag="gap")
+                terms = (floor, neg_h1, neg_old)
+                for k, term in enumerate(terms):
+                    for b in range(BLOCKS):
+                        nc.tensor.matmul(
+                            out=gap_bank[:, b * P : (b + 1) * P],
+                            lhsT=term[:, half * BANK + b * P : half * BANK + (b + 1) * P],
+                            rhs=ident[:],
+                            is_transpose=True,
+                            start=(k == 0 and b == 0),
+                            stop=(k == len(terms) - 1 and b == BLOCKS - 1),
+                        )
+                excess_turned = ring.tile([P, BANK], F32, name="excess_turned", tag="excess_turned")
+                nc.scalar.activation(out=excess_turned[:], in_=gap_bank[:], func=RELU, scale=-1.0)
+                back_bank = psum.tile([P, BANK], F32, name="back_bank", tag="back")
+                for b in range(BLOCKS):
+                    nc.tensor.transpose(back_bank[:, b * P : (b + 1) * P], excess_turned[:, b * P : (b + 1) * P], ident[:])
+                nc.scalar.copy(out=excess[:, cols], in_=back_bank[:])
+            pieces = HALVES if t == 0 else 1
+            for piece in range(pieces):
+                width = S // pieces
+                cols = slice(piece * width, (piece + 1) * width)
                 nc.vector.tensor_tensor(
-                    out=summed[:, cols],
-                    in0=page[t][:].indirect(list_part(put_list, half * BANK, BANK)),
-                    in1=h1[:, cols],
+                    out=page[t][:].indirect(list_part(put_list, piece * width, width)),
+                    in0=excess[:, cols],
+                    in1=floor[:, cols],
                     op=ADD,
                 )
-            for half in range(HALVES):
-                cols = slice(half * BANK, (half + 1) * BANK)
-                nc.vector.scalar_tensor_tensor(
-                    out=fresh[:, cols],
-                    in0=h2_banks[half][:],
-                    scalar=b2_col[:, t : t + 1],
-                    in1=summed[:, cols],
-                    op0=ADD,
-                    op1=MAX,
-                )
-            nc.vector.tensor_copy(out=page[t][:].indirect(put_list[:]), in_=fresh[:])
 
+        w3_w = ring.tile([P, N], U32, name="w3_w", tag="excess1", bufs=1, align_bytes=64)
         nc.scalar.copy(
             out=w3_bf[:].rearrange("p (c i j) -> p c j i", i=PACK, j=PACK),
             in_=w3_raw[:].rearrange("p (j c i) -> p c j i", i=PACK, j=PACK),
@@ -199,7 +226,7 @@ def tile_list_bin_habit_update_kernel(
 
         out_rows = out.rearrange("(c p) m -> p c m", p=P)
         for chunk in range(CHUNKS):
-            picked = ring.tile([P, PACK, CHUNK], F32, name="picked", tag=("summed", "fresh")[chunk % 2])
+            picked = ring.tile([P, PACK, CHUNK], F32, name="picked", tag=PICKED_TAGS[chunk], bufs=1, align_bytes=64)
             for t in range(PACK):
                 nc.vector.tensor_copy(
                     out=picked[:, t, :], in_=page[t][:].indirect(list_part(read_list, chunk * CHUNK, CHUNK))
@@ -213,8 +240,8 @@ def tile_list_bin_habit_update_kernel(
             )
             nc.vector.quantize_mx(out=x_w[:].bitcast(FP8X4), scales=x_s[:], in_=x_bf[:])
             for pair in range(N_TILES // 2):
-                y1_bank = psum.tile([P, 2, CHUNK], F32, name="y1_bank", tag="first")
-                y2_bank = psum.tile([P, 2, CHUNK], F32, name="y2_bank", tag="second")
+                y1_bank = psum.tile([P, 2, CHUNK], F32, name="y1_bank", tag=("h1", "gap")[pair % 2])
+                y2_bank = psum.tile([P, 2, CHUNK], F32, name="y2_bank", tag=("h2", "back")[pair % 2])
                 for bank, words, scales in ((y1_bank, w3_w, w3_s), (y2_bank, w4_w, w4_s)):
                     for side in range(2):
                         cols = slice((2 * pair + side) * P, (2 * pair + side + 1) * P)

from contextlib import ExitStack

import concourse.mybir as mybir
from concourse.masks import make_identity

K, H, N, T, S, T2, PICKS = 1024, 512, 768, 4096, 1024, 2048, 1024
FLOPS = 2 * 2 * K * H * S + 2 * 2 * H * N * PICKS

F32 = mybir.dt.float32
BF16 = mybir.dt.bfloat16
I32 = mybir.dt.int32
U32 = mybir.dt.uint32
U16 = mybir.dt.uint16
U8 = mybir.dt.uint8
FP8X4 = mybir.dt.float8_e4m3fn_x4
FP4X4 = mybir.dt.float4_e2m1fn_x4
ADD = mybir.AluOpType.add
MULT = mybir.AluOpType.mult
IDENTITY = mybir.ActivationFunctionType.Identity
COPY = mybir.ActivationFunctionType.Copy
RELU = mybir.ActivationFunctionType.Relu
TANH = mybir.ActivationFunctionType.Tanh

P = 128
PACK = 4
PASSES = K // (P * PACK)
BANK = 512
HALVES = S // BANK
BLOCKS = BANK // P
CHUNK = 256
CHUNKS = PICKS // CHUNK
N_TILES = N // P
PER_COL = 16
PICKED_TAGS = ("floor2", "excess2", "floor3", "floor2")


def tile_list_bin_habit_update_kernel(
    tc, tab_words, tab_scales, offs, offs2, offs3, w1, w2_words, w2_scales, b2, page0, w3, d, w4_words, w4_scales, out
):
    nc = tc.nc
    with ExitStack() as ctx:
        keep = ctx.enter_context(tc.tile_pool(name="keep", bufs=1))
        ring = ctx.enter_context(tc.tile_pool(name="ring", bufs=2))
        outs = ctx.enter_context(tc.tile_pool(name="outs", bufs=4))
        psum = ctx.enter_context(tc.psum_pool(name="psum", bufs=2))

        def held(shape, dtype, name):
            return keep.tile(shape, dtype, name=name, align_bytes=64)

        lift_list = held([P, S // PER_COL], U16, "lift_list")
        put_list = held([P, S // PER_COL], U16, "put_list")
        read_list = held([P, PICKS // PER_COL], U16, "read_list")
        tab_w = [held([P, T], I32, f"tab_w{a}") for a in range(PASSES)]
        tab_s = held([P, PASSES * T], U8, "tab_s")
        v_w = [held([P, S], U32, f"v_w{a}") for a in range(PASSES)]
        v_s = held([P, PASSES * S], U8, "v_s")
        w1_raw = [held([P, PACK * H], F32, f"w1_raw{a}") for a in range(PASSES)]
        w1_bf = [held([P, PACK * H], BF16, f"w1_bf{a}") for a in range(PASSES)]
        w1_w = [held([P, H], U32, f"w1_w{a}") for a in range(PASSES)]
        w1_s = [held([P, H], U8, f"w1_s{a}") for a in range(PASSES)]
        w2_raw_w = held([P, PASSES * 2 * H], U8, "w2_raw_w")
        w2_raw_s = held([P, PASSES * H], U8, "w2_raw_s")
        w2_w = held([P, PASSES * 2 * H], U8, "w2_w")
        w2_s = held([P, PASSES * H], U8, "w2_s")
        b2_col = held([P, PACK], F32, "b2_col")
        d_col = held([P, N_TILES], F32, "d_col")
        page = [held([P, T2], F32, f"page{t}") for t in range(PACK)]
        w3_raw = held([P, PACK * N], F32, "w3_raw")
        w3_bf = held([P, PACK * N], BF16, "w3_bf")
        w3_s = held([P, N], U8, "w3_s")
        w4_w = held([P, N], I32, "w4_w")
        w4_s = held([P, N], U8, "w4_s")

        ident = held([P, P], F32, "ident")

        nc.vector.memset(tab_s[:].bitcast(I32), 0)
        nc.gpsimd.memset(w2_raw_s[:].bitcast(I32), 0)
        nc.gpsimd.memset(w4_s[:].bitcast(I32), 0)
        make_identity(nc, ident[:])

        def load_scales(plane, scales):
            passes = scales.shape[0]
            for q in range(4):
                nc.sync.dma_start(
                    out=plane[32 * q : 32 * q + 4, :].bitcast(I32).rearrange("r (a n) -> r a n", a=passes),
                    in_=scales[:, 4 * q : 4 * q + 4, :].bitcast(I32).rearrange("a r n -> r a n"),
                )

        def load_table(a):
            nc.sync.dma_start(out=tab_w[a][:], in_=tab_words[a].rearrange("p n i -> p (n i)").bitcast(I32))

        nc.sync.dma_start(lift_list[:], offs)
        load_table(0)
        load_scales(tab_s, tab_scales)
        for a in range(PASSES):
            nc.sync.dma_start(
                out=w1_raw[a][:], in_=w1[a * P * PACK : (a + 1) * P * PACK, :].rearrange("(p j) c -> p (j c)", j=PACK)
            )
        nc.sync.dma_start(
            out=w2_raw_w[:].bitcast(I32).rearrange("p (a n) -> p a n", a=PASSES),
            in_=w2_words.bitcast(I32).rearrange("a p n -> p a n"),
        )
        load_scales(w2_raw_s, w2_scales)
        load_table(1)
        nc.sync.dma_start(put_list[:], offs2)
        nc.sync.dma_start(out=b2_col[:], in_=b2.rearrange("(p t) -> p t", t=PACK))
        page_rows = page0.rearrange("(p t) c -> p t c", t=PACK)
        for t in range(PACK):
            nc.sync.dma_start(out=page[t][:], in_=page_rows[:, t, :])
        nc.sync.dma_start(read_list[:], offs3)
        nc.sync.dma_start(out=w3_raw[:], in_=w3.rearrange("(p j) c -> p (j c)", j=PACK))
        nc.sync.dma_start(out=w4_w[:], in_=w4_words[0].rearrange("p n i -> p (n i)").bitcast(I32))
        load_scales(w4_s, w4_scales)
        with nc.allow_non_contiguous_dma(reason="one factor of d for each partition"):
            nc.sync.dma_start(out=d_col[:], in_=d.rearrange("(c p) -> p c", p=P))

        def list_part(lst, start, count):
            return lst[:, start // PER_COL : (start + count) // PER_COL]

        nc.vector.tensor_copy(out=v_w[0][:], in_=tab_w[0][:].bitcast(U32).indirect(lift_list[:]))
        for a in range(PASSES):
            nc.vector.tensor_copy(
                out=v_s[:, a * S : (a + 1) * S], in_=tab_s[:, a * T : (a + 1) * T].indirect(lift_list[:])
            )
        for a in range(PASSES):
            nc.scalar.copy(
                out=w1_bf[a][:].rearrange("p (t m j) -> p m t j", t=PACK, j=PACK),
                in_=w1_raw[a][:].rearrange("p (j m t) -> p m t j", t=PACK, j=PACK),
            )
            nc.vector.quantize_mx(out=w1_w[a][:].bitcast(FP8X4), scales=w1_s[a][:], in_=w1_bf[a][:])
        nc.vector.tensor_copy(
            out=w2_w[:].bitcast(U16).rearrange("p (a t m) -> p a t m", a=PASSES, t=PACK),
            in_=w2_raw_w[:].bitcast(U16).rearrange("p (a m t) -> p a t m", a=PASSES, t=PACK),
        )
        nc.vector.tensor_copy(
            out=w2_s[:].rearrange("p (a t m) -> p a t m", a=PASSES, t=PACK),
            in_=w2_raw_s[:].rearrange("p (a m t) -> p a t m", a=PASSES, t=PACK),
        )
        for half in range(HALVES):
            nc.vector.tensor_copy(
                out=v_w[1][:, half * BANK : (half + 1) * BANK],
                in_=tab_w[1][:].bitcast(U32).indirect(list_part(lift_list, half * BANK, BANK)),
            )

        for t in range(PACK):
            neg_old = ring.tile([P, S], F32, name="neg_old", tag="neg_old", bufs=PACK)
            neg_h1 = ring.tile([P, S], F32, name="neg_h1", tag="neg_h1")
            floor = ring.tile([P, S], F32, name="floor", tag=f"floor{t}", bufs=1, align_bytes=64)
            excess = ring.tile([P, S], F32, name="excess", tag=f"excess{t}", bufs=1, align_bytes=64)
            for half in range(HALVES):
                cols = slice(half * BANK, (half + 1) * BANK)
                nc.vector.tensor_scalar(
                    out=neg_old[:, cols],
                    in0=page[t][:].indirect(list_part(put_list, half * BANK, BANK)),
                    scalar1=-1.0,
                    scalar2=0.0,
                    op0=MULT,
                    op1=ADD,
                )
                h1_bank = psum.tile([P, BANK], F32, name="h1_bank", tag="h1")
                h2_bank = psum.tile([P, BANK], F32, name="h2_bank", tag="h2")
                for a in range(PASSES):
                    first = a * H + t * P
                    nc.tensor.matmul_mx(
                        out=h2_bank[:],
                        lhsT=w2_w[:, 2 * first : 2 * (first + P)].bitcast(FP4X4),
                        lhsT_scale=w2_s[:, first : first + P],
                        rhs=v_w[a][:, cols].bitcast(FP8X4),
                        rhs_scale=v_s[:, a * S + half * BANK : a * S + (half + 1) * BANK],
                        start=(a == 0),
                        stop=(a == PASSES - 1),
                    )
                for a in range(PASSES):
                    nc.tensor.matmul_mx(
                        out=h1_bank[:],
                        lhsT=w1_w[a][:, t * P : (t + 1) * P].bitcast(FP8X4),
                        lhsT_scale=w1_s[a][:, t * P : (t + 1) * P],
                        rhs=v_w[a][:, cols].bitcast(FP8X4),
                        rhs_scale=v_s[:, a * S + half * BANK : a * S + (half + 1) * BANK],
                        start=(a == 0),
                        stop=(a == PASSES - 1),
                    )
                nc.scalar.activation(out=floor[:, cols], in_=h2_bank[:], func=IDENTITY, bias=b2_col[:, t : t + 1])
                nc.scalar.activation(out=neg_h1[:, cols], in_=h1_bank[:], func=COPY, scale=-1.0)
                gap_bank = psum.tile([P, BANK], F32, name="gap_bank", tag="gap")
                terms = (floor, neg_h1, neg_old)
                for k, term in enumerate(terms):
                    for b in range(BLOCKS):
                        nc.tensor.matmul(
                            out=gap_bank[:, b * P : (b + 1) * P],
                            lhsT=term[:, half * BANK + b * P : half * BANK + (b + 1) * P],
                            rhs=ident[:],
                            is_transpose=True,
                            start=(k == 0 and b == 0),
                            stop=(k == len(terms) - 1 and b == BLOCKS - 1),
                        )
                excess_turned = ring.tile([P, BANK], F32, name="excess_turned", tag="excess_turned")
                nc.scalar.activation(out=excess_turned[:], in_=gap_bank[:], func=RELU, scale=-1.0)
                back_bank = psum.tile([P, BANK], F32, name="back_bank", tag="back")
                for b in range(BLOCKS):
                    nc.tensor.transpose(back_bank[:, b * P : (b + 1) * P], excess_turned[:, b * P : (b + 1) * P], ident[:])
                nc.scalar.copy(out=excess[:, cols], in_=back_bank[:])
            pieces = HALVES if t == 0 else 1
            for piece in range(pieces):
                width = S // pieces
                cols = slice(piece * width, (piece + 1) * width)
                nc.vector.tensor_tensor(
                    out=page[t][:].indirect(list_part(put_list, piece * width, width)),
                    in0=excess[:, cols],
                    in1=floor[:, cols],
                    op=ADD,
                )

        w3_w = ring.tile([P, N], U32, name="w3_w", tag="excess1", bufs=1, align_bytes=64)
        nc.scalar.copy(
            out=w3_bf[:].rearrange("p (c i j) -> p c j i", i=PACK, j=PACK),
            in_=w3_raw[:].rearrange("p (j c i) -> p c j i", i=PACK, j=PACK),
        )
        for part in range(2):
            cols = slice(part * N // 2, (part + 1) * N // 2)
            nc.vector.quantize_mx(
                out=w3_w[:, cols].bitcast(FP8X4),
                scales=w3_s[:, cols],
                in_=w3_bf[:, part * PACK * N // 2 : (part + 1) * PACK * N // 2],
            )

        out_rows = out.rearrange("(c p) m -> p c m", p=P)
        for chunk in range(CHUNKS):
            picked = ring.tile([P, PACK, CHUNK], F32, name="picked", tag=PICKED_TAGS[chunk], bufs=1, align_bytes=64)
            for t in range(PACK):
                nc.vector.tensor_copy(
                    out=picked[:, t, :], in_=page[t][:].indirect(list_part(read_list, chunk * CHUNK, CHUNK))
                )
            x_bf = ring.tile([P, CHUNK * PACK], BF16, name="x_bf", tag="x_bf", align_bytes=64)
            x_w = ring.tile([P, CHUNK], U32, name="x_w", tag="x_w", align_bytes=64)
            x_s = ring.tile([P, CHUNK], U8, name="x_s", tag="x_s", align_bytes=64)
            nc.scalar.copy(
                out=x_bf[:].rearrange("p (c i t) -> p c t i", i=PACK, t=PACK),
                in_=picked[:].rearrange("p t (c i) -> p c t i", i=PACK),
            )
            nc.vector.quantize_mx(out=x_w[:].bitcast(FP8X4), scales=x_s[:], in_=x_bf[:])
            for pair in range(N_TILES // 2):
                y1_bank = psum.tile([P, 2, CHUNK], F32, name="y1_bank", tag=("h1", "gap")[pair % 2])
                y2_bank = psum.tile([P, 2, CHUNK], F32, name="y2_bank", tag=("h2", "back")[pair % 2])
                for bank, words, scales in ((y1_bank, w3_w, w3_s), (y2_bank, w4_w, w4_s)):
                    for side in range(2):
                        cols = slice((2 * pair + side) * P, (2 * pair + side + 1) * P)
                        nc.tensor.matmul_mx(
                            out=bank[:, side, :],
                            lhsT=words[:, cols].bitcast(FP8X4),
                            lhsT_scale=scales[:, cols],
                            rhs=x_w[:].bitcast(FP8X4),
                            rhs_scale=x_s[:],
                            start=True,
                            stop=True,
                        )
                squashed = outs.tile([P, 2, CHUNK], F32, name="squashed", tag="squashed")
                result = outs.tile([P, 2, CHUNK], F32, name="result", tag="result")
                nc.scalar.activation(out=squashed[:], in_=y1_bank[:], func=TANH)
                for side in range(2):
                    nc.vector.scalar_tensor_tensor(
                        out=result[:, side, :],
                        in0=squashed[:, side, :],
                        scalar=d_col[:, 2 * pair + side : 2 * pair + side + 1],
                        in1=y2_bank[:, side, :],
                        op0=MULT,
                        op1=ADD,
                    )
                nc.sync.dma_start(
                    out=out_rows[:, 2 * pair : 2 * pair + 2, chunk * CHUNK : (chunk + 1) * CHUNK], in_=result[:]
                )
